import numpy as np
import ml_dtypes


def mxq(x, axis, fmt="e4m3"):
    dtype, down = {"e4m3": (ml_dtypes.float8_e4m3fn, 7), "e5m2": (ml_dtypes.float8_e5m2, 14)}[fmt]
    v = np.moveaxis(np.asarray(x, np.float32).astype(ml_dtypes.bfloat16).astype(np.float64), axis, -1)
    blocks = v.reshape(v.shape[:-1] + (-1, 32))
    amax = np.abs(blocks).max(-1, keepdims=True)
    byte = np.maximum(np.where(amax > 0, np.frexp(amax)[1] - 1 + 127, 0) - down, 1)
    scale = np.exp2(byte - 127.0)
    codes = (blocks / scale).astype(np.float32).astype(dtype).astype(np.float64)
    return np.moveaxis((codes * scale).reshape(v.shape), -1, axis)


WIDE = False


def mx_kscale(k):
    if not WIDE:
        return np.ones(k)
    levels = np.array([30, -30])
    if k % 512:
        return np.exp2(np.random.permutation(np.resize(levels, k // 32))).repeat(32)
    a = np.empty((k // 512, 16))
    for p in range(k // 512):
        a[p, :8] = np.random.permutation(np.resize(levels, 8))
        for g in range(8):
            far = levels[np.abs(levels - a[p, g]) >= 10]
            a[p, g + 8] = far[np.random.randint(len(far))]
    return np.exp2(a.ravel()).repeat(32)


def f64(x):
    return np.asarray(x).astype(np.float64)


def striped(idx):
    return np.tile(idx.reshape(-1, 16).T, (8, 1)).astype(np.uint16)


def unstriped(offs):
    return offs[:16].T.reshape(-1).astype(np.int64)


E2M1 = np.array([0.0, 0.5, 1.0, 1.5, 2.0, 3.0, 4.0, 6.0, -0.0, -0.5, -1.0, -1.5, -2.0, -3.0, -4.0, -6.0])


def pack_weight(w, fmt):
    k, n = w.shape
    w = f64(np.asarray(w, np.float32).astype(ml_dtypes.bfloat16)).reshape(k // 32, 32, n)
    amax = np.abs(w).max(1)
    if fmt == "e4m3":
        byte = np.frexp(amax)[1] - 1 + 127 - 7
    elif fmt == "e5m2":
        byte = np.frexp(amax)[1] - 1 + 127 - 14
    else:
        mant, ex = np.frexp(amax / 6.0)
        byte = np.where(mant > 0.5, ex, ex - 1) + 127
    byte = np.clip(np.where(amax > 0, byte, 1), 1, 254)
    scaled = (w * np.exp2(127.0 - byte)[:, None, :]).reshape(k, n).astype(np.float32)
    by_word = np.ascontiguousarray(scaled.reshape(k // 512, 128, 4, n).transpose(0, 1, 3, 2))
    if fmt == "e4m3":
        words = by_word.astype(ml_dtypes.float8_e4m3fn).view(np.uint8)
    elif fmt == "e5m2":
        words = by_word.astype(ml_dtypes.float8_e5m2).view(np.uint8)
    else:
        c = by_word.astype(ml_dtypes.float4_e2m1fn).view(np.uint8) & 0xF
        words = (c[..., 0::2] | (c[..., 1::2] << 4)).reshape(k // 512, 128, 2 * n)
    return np.ascontiguousarray(words), np.ascontiguousarray(byte.astype(np.uint8).reshape(k // 512, 16, n))


def unpack_weight(words, scales, fmt):
    g, _, n = scales.shape
    words = np.ascontiguousarray(words).reshape(g, 128, n, -1)
    if fmt == "e4m3":
        vals = words.view(ml_dtypes.float8_e4m3fn).astype(np.float64)
    elif fmt == "e5m2":
        vals = words.view(ml_dtypes.float8_e5m2).astype(np.float64)
    else:
        nib = np.empty((g, 128, n, 4), np.uint8)
        nib[..., 0::2] = words & 0xF
        nib[..., 1::2] = words >> 4
        vals = E2M1[nib]
    vals = vals * np.repeat(np.exp2(scales.astype(np.float64) - 127.0), 8, axis=1)[..., None]
    return vals.transpose(0, 1, 3, 2).reshape(g * 512, n)


def d_relu2(v):
    return 2.0 * np.maximum(v, 0.0)


K, T, E, C, H, N = 256, 1536, 6, 512, 512, 512


def by_expert(wq, xq):
    return np.concatenate([wq[e].T @ xq[:, e * C:(e + 1) * C] for e in range(E)], axis=1)


def setup_inputs():
    n = np.random.standard_normal
    v = mx_kscale(N)
    u = mx_kscale(H)
    first = np.random.permutation(np.repeat(np.arange(E), T // E))
    second = (first + 1 + np.random.permutation(np.repeat(np.arange(E - 1), -(-T // (E - 1)))[:T])) % E
    while np.bincount(second, minlength=E).max() != T // E:
        load = np.bincount(second, minlength=E); hi, lo = int(load.argmax()), int(load.argmin())
        t = np.flatnonzero((second == hi) & (first != lo))[0]; second[t] = lo
    slot_token = np.empty(E * C, np.int64); pos = np.empty((2, T), np.int64); fill = np.zeros(E, np.int64)
    place = np.stack([np.random.permutation(C) for _ in range(E)])
    for r, deal in enumerate((first, second)):
        for t in np.random.permutation(T):
            e = deal[t]; j = e * C + place[e, fill[e]]; fill[e] += 1; slot_token[j] = t; pos[r, t] = j
    g = np.random.uniform(0.2, 0.8, T)
    dy = pack_weight(n((N, T)) * v[:, None], "e5m2")
    w2t = [pack_weight(m, "e2m1") for m in n((E, N, H)) / np.sqrt(N) / v[None, :, None] * u]
    w1t = pack_weight(n((H, K)) / np.sqrt(H) / u[:, None], "e2m1")
    return {
        "dy_words": dy[0],
        "dy_scales": dy[1],
        "w2t_words": np.stack([m[0] for m in w2t]),
        "w2t_scales": np.stack([m[1] for m in w2t]),
        "w1t_words": w1t[0],
        "w1t_scales": w1t[1],
        "a": (n((H, T))).astype(np.float32),
        "gate": np.stack([np.tile(g, (128, 1)), np.tile(1.0 - g, (128, 1))]).astype(np.float32),
        "offs": striped(slot_token),
        "pos1": striped(pos[0]),
        "pos2": striped(pos[1]),
    }


def reference(dy_words, dy_scales, w2t_words, w2t_scales, w1t_words, w1t_scales, a, gate, offs, pos1, pos2):
    w2t = np.stack([unpack_weight(w2t_words[e], w2t_scales[e], "e2m1") for e in range(E)])
    w1t = unpack_weight(w1t_words, w1t_scales, "e2m1")
    idx = unstriped(offs)
    gq = unpack_weight(dy_words, dy_scales, "e5m2")[:, idx]
    y = by_expert(w2t, gq)
    dh = sum(f64(gate[r, :1]) * y[:, unstriped(p)] for r, p in enumerate((pos1, pos2)))
    return w1t.T @ mxq(dh * d_relu2(f64(a)), 0, "e5m2")

@@ -1,0 +1,187 @@
+from contextlib import ExitStack
+
+import concourse.mybir as mybir
+from concourse.masks import make_identity
+
+K, T, E, C, H, N = 256, 1536, 6, 512, 512, 512
+SLOTS = E * C
+FLOPS = 2 * N * H * SLOTS + 2 * H * K * T
+
+F32 = mybir.dt.float32
+BF16 = mybir.dt.bfloat16
+I32 = mybir.dt.int32
+U32 = mybir.dt.uint32
+U16 = mybir.dt.uint16
+U8 = mybir.dt.uint8
+E5M2 = mybir.dt.float8_e5m2_x4
+E2M1 = mybir.dt.float4_e2m1fn_x4
+ALU = mybir.AluOpType
+COPY = mybir.ActivationFunctionType.Copy
+
+P = 128
+PACK = 4
+BANK = 512
+LIST_ROWS = 16
+BLOCKS = T // P
+GROUPS = (256, 256, 256, 256, 256, 128, 128)
+F32_MAX = 3.4028234663852886e38
+
+
+def load_scale_rows(queue, plane, rows):
+    for r in range(4):
+        queue.dma_start(out=plane[r:P:32].bitcast(I32), in_=rows[r:16:4].bitcast(I32))
+
+
+def tile_moe_sub_relu2_kernel(
+    tc, dy_words, dy_scales, w2t_words, w2t_scales, w1t_words, w1t_scales, a, gate, offs, pos1, pos2, out
+):
+    nc = tc.nc
+    with ExitStack() as ctx:
+        keep = ctx.enter_context(tc.tile_pool(name="keep", bufs=1))
+        ring = ctx.enter_context(tc.tile_pool(name="ring", bufs=1))
+        psum = ctx.enter_context(tc.psum_pool(name="psum", bufs=1))
+
+        offs_sb = keep.tile([P, SLOTS // LIST_ROWS], U16)
+        pos_sb = [keep.tile([P, T // LIST_ROWS], U16, name=f"pos{r}") for r in range(2)]
+        dy_w = keep.tile([P, T], I32, align_bytes=64)
+        dy_s = keep.tile([P, T], U8, align_bytes=64)
+        w2_w = keep.tile([P, E, 2 * H], U8, align_bytes=64)
+        w2_s = keep.tile([P, E, H], U8, align_bytes=64)
+        w1_w = keep.tile([P, 2 * K], U8, align_bytes=64)
+        w1_s = keep.tile([P, K], U8, align_bytes=64)
+        gate_rows = keep.tile([P, P], F32, tag="gate_then_a")
+        gate_cols = keep.tile([P, 2 * BLOCKS], F32)
+        ident = keep.tile([P, P], F32)
+
+        nc.gpsimd.memset(dy_s[:].bitcast(I32), 0)
+        nc.vector.memset(w2_s[:].bitcast(I32), 0)
+        nc.vector.memset(w1_s[:].bitcast(I32), 0)
+        nc.gpsimd.memset(gate_rows[:], 0.0)
+
+        nc.sync.dma_start(offs_sb[:], offs)
+        nc.sync.dma_start(out=dy_w[:], in_=dy_words[0].rearrange("p t d -> p (t d)").bitcast(I32))
+        load_scale_rows(nc.sync, dy_s[:], dy_scales[0])
+        nc.sync.dma_start(out=w2_w[:].bitcast(I32), in_=w2t_words[:, 0].rearrange("e p c -> p e c").bitcast(I32))
+        for r in range(2):
+            nc.gpsimd.dma_start(
+                out=gate_rows[r * BLOCKS : (r + 1) * BLOCKS, :], in_=gate[r, 0].rearrange("(b t) -> b t", t=P)
+            )
+        make_identity(nc, ident[:])
+        load_scale_rows(nc.sync, w2_s[:], w2t_scales[:, 0].rearrange("e b i -> b e i"))
+        nc.sync.dma_start(pos_sb[0][:], pos1)
+        nc.sync.dma_start(pos_sb[1][:], pos2)
+        nc.gpsimd.dma_start(out=w1_w[:].bitcast(I32), in_=w1t_words[0].bitcast(I32))
+        load_scale_rows(nc.gpsimd, w1_s[:], w1t_scales[0])
+
+        gate_bank = psum.tile([P, BANK], F32, tag="out", bufs=2)
+        nc.tensor.transpose(gate_bank[:, :P], gate_rows[:], ident[:])
+        nc.scalar.activation(gate_cols[:], gate_bank[:, : 2 * BLOCKS], COPY, scale=2.0)
+
+        starts = [sum(GROUPS[:g]) for g in range(len(GROUPS))]
+        a_sb = keep.tile([P, PACK * T], F32, tag="gate_then_a")
+        relu_a = []
+        for g, width in enumerate(GROUPS):
+            a_g = a_sb[:, PACK * starts[g] : PACK * (starts[g] + width)].rearrange("p (m t) -> p m t", m=PACK)
+            nc.sync.dma_start(out=a_g, in_=a[:, starts[g] : starts[g] + width].rearrange("(m p) t -> p m t", p=P))
+            relu_g = keep.tile([P, PACK, width], F32, name=f"relu{g}")
+            nc.gpsimd.tensor_scalar(relu_g[:], a_g, F32_MAX, 0.0, ALU.min, ALU.max)
+            relu_a.append(relu_g)
+
+        y = [keep.tile([P, SLOTS], F32, name=f"y{m}") for m in range(PACK)]
+        slot_w, slot_s = [], []
+
+        def gather_expert(e):
+            slot_list = offs_sb[:, e * C // LIST_ROWS : (e + 1) * C // LIST_ROWS]
+            words = ring.tile([P, C], U32, tag="slot_w", bufs=2, align_bytes=64)
+            scales = keep.tile([P, C], U8, name=f"slot_s{e}", align_bytes=64)
+            nc.vector.tensor_copy(words[:], dy_w[:].bitcast(U32).indirect(slot_list))
+            nc.vector.tensor_copy(scales[:], dy_s[:].indirect(slot_list))
+            slot_w.append(words)
+            slot_s.append(scales)
+
+        def expert_rows(e, m):
+            y_bank = psum.tile([P, BANK], F32, tag="turned", bufs=4)
+            nc.tensor.matmul_mx(
+                y_bank[:],
+                lhsT=w2_w[:, e, 2 * P * m : 2 * P * (m + 1)].bitcast(E2M1),
+                lhsT_scale=w2_s[:, e, P * m : P * (m + 1)],
+                rhs=slot_w[e][:].bitcast(E5M2),
+                rhs_scale=slot_s[e][:],
+                start=True,
+                stop=True,
+            )
+            nc.scalar.copy(y[m][:, e * C : (e + 1) * C], y_bank[:])
+
+        for e in range(E - 2):
+            gather_expert(e)
+            for m in range(PACK):
+                expert_rows(e, m)
+        gather_expert(E - 2)
+        gather_expert(E - 1)
+        for m in range(PACK):
+            expert_rows(E - 2, m)
+            expert_rows(E - 1, m)
+
+        da_w = keep.tile([P, T], U32, align_bytes=64)
+        da_s = keep.tile([P, T], U8, align_bytes=64)
+        for g, width in enumerate(GROUPS):
+            start = starts[g]
+            scaled = {}
+            for r in range(2):
+                token_list = pos_sb[r][:, start // LIST_ROWS : (start + width) // LIST_ROWS]
+                picked = ring.tile([P, PACK, width], F32, tag=f"picked{r}", bufs=1)
+                turned = [
+                    psum.tile([P, BANK], F32, tag="turned", bufs=4, name=f"turned{b}") for b in range(width // P)
+                ]
+                for m in range(PACK):
+                    nc.vector.tensor_tensor(picked[:, m, :], y[m][:].indirect(token_list), relu_a[g][:, m, :], ALU.mult)
+                    for b in range(width // P):
+                        nc.tensor.transpose(turned[b][:, P * m : P * (m + 1)], picked[:, m, P * b : P * (b + 1)], ident[:])
+                for b in range(width // P):
+                    scaled_b = ring.tile([P, PACK, P], F32, tag="scaled", bufs=8)
+                    column = r * BLOCKS + start // P + b
+                    nc.scalar.activation(
+                        scaled_b[:],
+                        turned[b][:].rearrange("p (q d) -> p d q", d=PACK),
+                        COPY,
+                        scale=gate_cols[:, column : column + 1],
+                    )
+                    scaled[r, b] = scaled_b
+            da = ring.tile([P, width, PACK], BF16, tag="da", bufs=3, align_bytes=64)
+            for b in range(width // P):
+                summed = psum.tile([P, BANK], F32, tag="summed", bufs=2)
+                for d in range(PACK):
+                    for r in range(2):
+                        nc.tensor.matmul(
+                            summed[:, P * d : P * (d + 1)],
+                            lhsT=scaled[r, b][:, d, :],
+                            rhs=ident[:],
+                            is_transpose=True,
+                            start=(r == 0),
+                            stop=(r == 1),
+                        )
+                nc.scalar.copy(da[:, P * b : P * (b + 1), :], summed[:].rearrange("p (d t) -> p t d", d=PACK))
+            nc.vector.quantize_mx(
+                out=da_w[:, start : start + width].bitcast(E5M2),
+                scales=da_s[:, start : start + width],
+                in_=da[:].rearrange("p t d -> p (t d)"),
+            )
+            end = start + width
+            if end % BANK == 0:
+                for h in range(K // P):
+                    out_bank = psum.tile([P, BANK], F32, tag="out", bufs=2)
+                    nc.tensor.matmul_mx(
+                        out_bank[:],
+                        lhsT=w1_w[:, 2 * P * h : 2 * P * (h + 1)].bitcast(E2M1),
+                        lhsT_scale=w1_s[:, P * h : P * (h + 1)],
+                        rhs=da_w[:, end - BANK : end].bitcast(E5M2),
+                        rhs_scale=da_s[:, end - BANK : end],
+                        start=True,
+                        stop=True,
+                    )
+                    staged = ring.tile([P, BANK], F32, tag="staged", bufs=4)
+                    if end == T and h == 1:
+                        nc.vector.tensor_copy(staged[:], out_bank[:])
+                    else:
+                        nc.scalar.copy(staged[:], out_bank[:])
+                    nc.sync.dma_start(out=out[P * h : P * (h + 1), end - BANK : end], in_=staged[:])

@@ -24,7 +24,8 @@ BANK = 512
 LIST_ROWS = 16
 BLOCKS = T // P
 GROUPS = (256, 256, 256, 256, 256, 128, 128)
-F32_MAX = 3.4028234663852886e38
+GATE_FIRST = (True, False, False, True, False, False, True)
+RELU = mybir.ActivationFunctionType.Relu
 
 
 def load_scale_rows(queue, plane, rows):
@@ -75,17 +76,25 @@ def tile_moe_sub_relu2_kernel(
 
         gate_bank = psum.tile([P, BANK], F32, tag="out", bufs=2)
         nc.tensor.transpose(gate_bank[:, :P], gate_rows[:], ident[:])
-        nc.scalar.activation(gate_cols[:], gate_bank[:, : 2 * BLOCKS], COPY, scale=2.0)
+        nc.scalar.activation(gate_cols[:], gate_bank[:, : 2 * BLOCKS], COPY)
 
         starts = [sum(GROUPS[:g]) for g in range(len(GROUPS))]
-        a_sb = keep.tile([P, PACK * T], F32, tag="gate_then_a")
-        relu_a = []
+        gate_width = sum(width for g, width in enumerate(GROUPS) if GATE_FIRST[g])
+        held = keep.tile([P, PACK * T + 2 * gate_width], F32, tag="gate_then_a")
+        a_sb, gate_sb = [], {}
+        used = PACK * T
         for g, width in enumerate(GROUPS):
-            a_g = a_sb[:, PACK * starts[g] : PACK * (starts[g] + width)].rearrange("p (m t) -> p m t", m=PACK)
-            nc.sync.dma_start(out=a_g, in_=a[:, starts[g] : starts[g] + width].rearrange("(m p) t -> p m t", p=P))
-            relu_g = keep.tile([P, PACK, width], F32, name=f"relu{g}")
-            nc.gpsimd.tensor_scalar(relu_g[:], a_g, F32_MAX, 0.0, ALU.min, ALU.max)
-            relu_a.append(relu_g)
+            tokens = slice(starts[g], starts[g] + width)
+            a_g = held[:, PACK * starts[g] : PACK * (starts[g] + width)].rearrange("p (m t) -> p m t", m=PACK)
+            if GATE_FIRST[g]:
+                gate_g = held[:, used : used + 2 * width].rearrange("p (r t) -> p r t", r=2)
+                nc.sync.dma_start(out=gate_g, in_=gate[:, :, tokens].rearrange("r p t -> p r t"))
+                gate_sb[g] = gate_g
+                used = used + 2 * width
+                nc.sync.dma_start(out=a_g, in_=a[:, tokens].rearrange("(p d) t -> p d t", d=PACK))
+            else:
+                nc.sync.dma_start(out=a_g, in_=a[:, tokens].rearrange("(m p) t -> p m t", p=P))
+            a_sb.append(a_g)
 
         y = [keep.tile([P, SLOTS], F32, name=f"y{m}") for m in range(PACK)]
         slot_w, slot_s = [], []
@@ -93,7 +102,7 @@ def tile_moe_sub_relu2_kernel(
         def gather_expert(e):
             slot_list = offs_sb[:, e * C // LIST_ROWS : (e + 1) * C // LIST_ROWS]
             words = ring.tile([P, C], U32, tag="slot_w", bufs=2, align_bytes=64)
-            scales = keep.tile([P, C], U8, name=f"slot_s{e}", align_bytes=64)
+            scales = keep.tile([P, C], U8, name=f"slot_s{e}", tag=f"slot_s{e}", align_bytes=64)
             nc.vector.tensor_copy(words[:], dy_w[:].bitcast(U32).indirect(slot_list))
             nc.vector.tensor_copy(scales[:], dy_s[:].indirect(slot_list))
             slot_w.append(words)
@@ -124,22 +133,62 @@ def tile_moe_sub_relu2_kernel(
 
         da_w = keep.tile([P, T], U32, align_bytes=64)
         da_s = keep.tile([P, T], U8, align_bytes=64)
-        for g, width in enumerate(GROUPS):
-            start = starts[g]
+        slope = {}
+
+        def make_slope(g):
+            width = GROUPS[g]
+            if GATE_FIRST[g]:
+                slope_g = keep.tile([P, width, PACK], F32, tag=f"slot_s{E - 1}", align_bytes=64)
+                nc.scalar.activation(slope_g[:], a_sb[g].rearrange("p d t -> p t d"), RELU, scale=2.0)
+            else:
+                slope_g = ring.tile([P, PACK, width], F32, tag="slot_w", bufs=2, align_bytes=64)
+                nc.scalar.activation(slope_g[:], a_sb[g], RELU, scale=2.0)
+            slope[g] = slope_g
+
+        def pick(g, r, m, factor):
+            token_list = pos_sb[r][:, starts[g] // LIST_ROWS : (starts[g] + GROUPS[g]) // LIST_ROWS]
+            picked = ring.tile([P, GROUPS[g]], F32, tag=f"picked{r}{m}", bufs=1)
+            nc.vector.tensor_tensor(picked[:], y[m][:].indirect(token_list), factor, ALU.mult)
+            return picked
+
+        def transpose_add(target, source, first, last):
+            nc.tensor.matmul(target, lhsT=source, rhs=ident[:], is_transpose=True, start=first, stop=last)
+
+        def combine_gate_first(g, da):
+            width = GROUPS[g]
+            turned = [psum.tile([P, BANK], F32, tag="turned", bufs=4, name=f"turned{b}") for b in range(width // P)]
+            for m in range(PACK):
+                picked = [pick(g, r, m, gate_sb[g][:, r, :]) for r in range(2)]
+                for b in range(width // P):
+                    for r in range(2):
+                        transpose_add(
+                            turned[b][:, P * m : P * (m + 1)], picked[r][:, P * b : P * (b + 1)], r == 0, r == 1
+                        )
+            for b in range(width // P):
+                dh = ring.tile([P, PACK, P], F32, tag="scaled", bufs=8)
+                nc.scalar.copy(dh[:], turned[b][:].rearrange("p (q d) -> p d q", d=PACK))
+                summed = psum.tile([P, BANK], F32, tag="summed", bufs=2)
+                for d in range(PACK):
+                    nc.tensor.transpose(summed[:, P * d : P * (d + 1)], dh[:, d, :], ident[:])
+                nc.vector.tensor_tensor(
+                    da[:, P * b : P * (b + 1), :],
+                    summed[:].rearrange("p (d t) -> p t d", d=PACK),
+                    slope[g][:, P * b : P * (b + 1), :],
+                    ALU.mult,
+                )
+
+        def combine_slope_first(g, da):
+            width = GROUPS[g]
             scaled = {}
             for r in range(2):
-                token_list = pos_sb[r][:, start // LIST_ROWS : (start + width) // LIST_ROWS]
-                picked = ring.tile([P, PACK, width], F32, tag=f"picked{r}", bufs=1)
-                turned = [
-                    psum.tile([P, BANK], F32, tag="turned", bufs=4, name=f"turned{b}") for b in range(width // P)
-                ]
+                turned = [psum.tile([P, BANK], F32, tag="turned", bufs=4, name=f"turned{b}") for b in range(width // P)]
                 for m in range(PACK):
-                    nc.vector.tensor_tensor(picked[:, m, :], y[m][:].indirect(token_list), relu_a[g][:, m, :], ALU.mult)
+                    picked = pick(g, r, m, slope[g][:, m, :])
                     for b in range(width // P):
-                        nc.tensor.transpose(turned[b][:, P * m : P * (m + 1)], picked[:, m, P * b : P * (b + 1)], ident[:])
+                        nc.tensor.transpose(turned[b][:, P * m : P * (m + 1)], picked[:, P * b : P * (b + 1)], ident[:])
                 for b in range(width // P):
                     scaled_b = ring.tile([P, PACK, P], F32, tag="scaled", bufs=8)
-                    column = r * BLOCKS + start // P + b
+                    column = r * BLOCKS + starts[g] // P + b
                     nc.scalar.activation(
                         scaled_b[:],
                         turned[b][:].rearrange("p (q d) -> p d q", d=PACK),
@@ -147,41 +196,51 @@ def tile_moe_sub_relu2_kernel(
                         scale=gate_cols[:, column : column + 1],
                     )
                     scaled[r, b] = scaled_b
-            da = ring.tile([P, width, PACK], BF16, tag="da", bufs=3, align_bytes=64)
             for b in range(width // P):
                 summed = psum.tile([P, BANK], F32, tag="summed", bufs=2)
                 for d in range(PACK):
                     for r in range(2):
-                        nc.tensor.matmul(
-                            summed[:, P * d : P * (d + 1)],
-                            lhsT=scaled[r, b][:, d, :],
-                            rhs=ident[:],
-                            is_transpose=True,
-                            start=(r == 0),
-                            stop=(r == 1),
-                        )
+                        transpose_add(summed[:, P * d : P * (d + 1)], scaled[r, b][:, d, :], r == 0, r == 1)
                 nc.scalar.copy(da[:, P * b : P * (b + 1), :], summed[:].rearrange("p (d t) -> p t d", d=PACK))
+
+        def project(first, end):
+            width = end - first
+            staged = ring.tile([P, K // P, width], F32, tag="staged", bufs=2)
+            for h in range(K // P):
+                out_bank = psum.tile([P, BANK], F32, tag="out", bufs=2)
+                nc.tensor.matmul_mx(
+                    out_bank[:],
+                    lhsT=w1_w[:, 2 * P * h : 2 * P * (h + 1)].bitcast(E2M1),
+                    lhsT_scale=w1_s[:, P * h : P * (h + 1)],
+                    rhs=da_w[:, end - BANK : end].bitcast(E5M2),
+                    rhs_scale=da_s[:, end - BANK : end],
+                    start=True,
+                    stop=True,
+                )
+                if end == T and h == 1:
+                    nc.vector.tensor_copy(staged[:, h, :], out_bank[:, BANK - width :])
+                else:
+                    nc.scalar.copy(staged[:, h, :], out_bank[:, BANK - width :])
+            nc.sync.dma_start(out=out[:, first:end].rearrange("(h p) t -> p h t", p=P), in_=staged[:])
+
+        stored = 0
+        for g, width in enumerate(GROUPS):
+            start = starts[g]
+            end = start + width
+            if g + 1 < len(GROUPS) and not GATE_FIRST[g + 1]:
+                make_slope(g + 1)
+            if GATE_FIRST[g]:
+                make_slope(g)
+            da = ring.tile([P, width, PACK], BF16, tag="da", bufs=3, align_bytes=64)
+            if GATE_FIRST[g]:
+                combine_gate_first(g, da)
+            else:
+                combine_slope_first(g, da)
             nc.vector.quantize_mx(
-                out=da_w[:, start : start + width].bitcast(E5M2),
-                scales=da_s[:, start : start + width],
+                out=da_w[:, start:end].bitcast(E5M2),
+                scales=da_s[:, start:end],
                 in_=da[:].rearrange("p t d -> p (t d)"),
             )
-            end = start + width
-            if end % BANK == 0:
-                for h in range(K // P):
-                    out_bank = psum.tile([P, BANK], F32, tag="out", bufs=2)
-                    nc.tensor.matmul_mx(
-                        out_bank[:],
-                        lhsT=w1_w[:, 2 * P * h : 2 * P * (h + 1)].bitcast(E2M1),
-                        lhsT_scale=w1_s[:, P * h : P * (h + 1)],
-                        rhs=da_w[:, end - BANK : end].bitcast(E5M2),
-                        rhs_scale=da_s[:, end - BANK : end],
-                        start=True,
-                        stop=True,
-                    )
-                    staged = ring.tile([P, BANK], F32, tag="staged", bufs=4)
-                    if end == T and h == 1:
-                        nc.vector.tensor_copy(staged[:], out_bank[:])
-                    else:
-                        nc.scalar.copy(staged[:], out_bank[:])
-                    nc.sync.dma_start(out=out[P * h : P * (h + 1), end - BANK : end], in_=staged[:])
+            if end % BANK == 0 or g == len(GROUPS) - 2:
+                project(stored, end)
+                stored = end

@@ -24,7 +24,11 @@ BANK = 512
 LIST_ROWS = 16
 BLOCKS = T // P
 GROUPS = (256, 256, 256, 256, 256, 128, 128)
-GATE_FIRST = (True, False, False, True, False, False, True)
+GATE_FIRST = (False, False, False, True, True, True, True)
+LAG = 3
+EARLY = 2
+NEARLY = 1
+PICK_BUFS = 2
 RELU = mybir.ActivationFunctionType.Relu
 
 
@@ -44,75 +48,65 @@ def tile_moe_sub_relu2_kernel(
 
         offs_sb = keep.tile([P, SLOTS // LIST_ROWS], U16)
         pos_sb = [keep.tile([P, T // LIST_ROWS], U16, name=f"pos{r}") for r in range(2)]
-        dy_w = keep.tile([P, T], I32, align_bytes=64)
+        dy_w = keep.tile([P, T], I32, tag="dy_then_slope", align_bytes=64)
         dy_s = keep.tile([P, T], U8, align_bytes=64)
-        w2_w = keep.tile([P, E, 2 * H], U8, align_bytes=64)
-        w2_s = keep.tile([P, E, H], U8, align_bytes=64)
-        w1_w = keep.tile([P, 2 * K], U8, align_bytes=64)
-        w1_s = keep.tile([P, K], U8, align_bytes=64)
-        gate_rows = keep.tile([P, P], F32, tag="gate_then_a")
+        w2_early = keep.tile([P, EARLY, 2 * H], U8, tag="words_then_a", align_bytes=64)
+        w_s = keep.tile([P, E * H + K], U8, align_bytes=64)
+        w2_s = w_s[:, : E * H].rearrange("p (e i) -> p e i", e=E)
+        w1_s = w_s[:, E * H :]
+        gate_rows = keep.tile([P, P], F32, tag="gate_then_words", align_bytes=64)
         gate_cols = keep.tile([P, 2 * BLOCKS], F32)
         ident = keep.tile([P, P], F32)
 
         nc.gpsimd.memset(dy_s[:].bitcast(I32), 0)
-        nc.vector.memset(w2_s[:].bitcast(I32), 0)
-        nc.vector.memset(w1_s[:].bitcast(I32), 0)
+        nc.vector.memset(w_s[:].bitcast(I32), 0)
         nc.gpsimd.memset(gate_rows[:], 0.0)
 
         nc.sync.dma_start(offs_sb[:], offs)
+        nc.sync.dma_start(pos_sb[0][:], pos1)
+        nc.sync.dma_start(pos_sb[1][:], pos2)
         nc.sync.dma_start(out=dy_w[:], in_=dy_words[0].rearrange("p t d -> p (t d)").bitcast(I32))
+        w2_rows = w2t_words[:, 0].rearrange("e p c -> p e c")
+        nc.sync.dma_start(out=w2_early[:].bitcast(I32), in_=w2_rows[:, :EARLY].bitcast(I32))
         load_scale_rows(nc.sync, dy_s[:], dy_scales[0])
-        nc.sync.dma_start(out=w2_w[:].bitcast(I32), in_=w2t_words[:, 0].rearrange("e p c -> p e c").bitcast(I32))
+        load_scale_rows(nc.sync, w2_s, w2t_scales[:, 0].rearrange("e b i -> b e i"))
         for r in range(2):
             nc.gpsimd.dma_start(
                 out=gate_rows[r * BLOCKS : (r + 1) * BLOCKS, :], in_=gate[r, 0].rearrange("(b t) -> b t", t=P)
             )
         make_identity(nc, ident[:])
-        load_scale_rows(nc.sync, w2_s[:], w2t_scales[:, 0].rearrange("e b i -> b e i"))
-        nc.sync.dma_start(pos_sb[0][:], pos1)
-        nc.sync.dma_start(pos_sb[1][:], pos2)
-        nc.gpsimd.dma_start(out=w1_w[:].bitcast(I32), in_=w1t_words[0].bitcast(I32))
-        load_scale_rows(nc.gpsimd, w1_s[:], w1t_scales[0])
 
-        gate_bank = psum.tile([P, BANK], F32, tag="out", bufs=2)
+        gate_bank = psum.tile([P, BANK], F32, tag="turned", bufs=4)
         nc.tensor.transpose(gate_bank[:, :P], gate_rows[:], ident[:])
         nc.scalar.activation(gate_cols[:], gate_bank[:, : 2 * BLOCKS], COPY)
 
-        starts = [sum(GROUPS[:g]) for g in range(len(GROUPS))]
-        gate_width = sum(width for g, width in enumerate(GROUPS) if GATE_FIRST[g])
-        held = keep.tile([P, PACK * T + 2 * gate_width], F32, tag="gate_then_a")
-        a_sb, gate_sb = [], {}
-        used = PACK * T
-        for g, width in enumerate(GROUPS):
-            tokens = slice(starts[g], starts[g] + width)
-            a_g = held[:, PACK * starts[g] : PACK * (starts[g] + width)].rearrange("p (m t) -> p m t", m=PACK)
-            if GATE_FIRST[g]:
-                gate_g = held[:, used : used + 2 * width].rearrange("p (r t) -> p r t", r=2)
-                nc.sync.dma_start(out=gate_g, in_=gate[:, :, tokens].rearrange("r p t -> p r t"))
-                gate_sb[g] = gate_g
-                used = used + 2 * width
-                nc.sync.dma_start(out=a_g, in_=a[:, tokens].rearrange("(p d) t -> p d t", d=PACK))
-            else:
-                nc.sync.dma_start(out=a_g, in_=a[:, tokens].rearrange("(m p) t -> p m t", p=P))
-            a_sb.append(a_g)
+        late_words = keep.tile([P, (E - EARLY) * 2 * H + 2 * K], U8, tag="gate_then_words", align_bytes=64)
+        w2_late = late_words[:, : (E - EARLY) * 2 * H].rearrange("p (e c) -> p e c", c=2 * H)
+        w1_w = late_words[:, (E - EARLY) * 2 * H :]
+        nc.sync.dma_start(out=w2_late.bitcast(I32), in_=w2_rows[:, EARLY:].bitcast(I32))
+        load_scale_rows(nc.sync, w1_s, w1t_scales[0])
+        nc.sync.dma_start(out=w1_w.bitcast(I32), in_=w1t_words[0].bitcast(I32))
+        w2_w = [w2_early[:, e, :] if e < EARLY else w2_late[:, e - EARLY, :] for e in range(E)]
 
-        y = [keep.tile([P, SLOTS], F32, name=f"y{m}") for m in range(PACK)]
+        starts = [sum(GROUPS[:g]) for g in range(len(GROUPS))]
+
+        y = [keep.tile([P, SLOTS], F32, name=f"y{m}", tag=f"y{m}", align_bytes=64) for m in range(PACK)]
         slot_w, slot_s = [], []
 
         def gather_expert(e):
             slot_list = offs_sb[:, e * C // LIST_ROWS : (e + 1) * C // LIST_ROWS]
             words = ring.tile([P, C], U32, tag="slot_w", bufs=2, align_bytes=64)
-            scales = keep.tile([P, C], U8, name=f"slot_s{e}", tag=f"slot_s{e}", align_bytes=64)
+            scales = ring.tile([P, C], U8, tag="slot_s", bufs=3, align_bytes=64)
             nc.vector.tensor_copy(words[:], dy_w[:].bitcast(U32).indirect(slot_list))
             nc.vector.tensor_copy(scales[:], dy_s[:].indirect(slot_list))
             slot_w.append(words)
             slot_s.append(scales)
 
         def expert_rows(e, m):
-            y_bank = psum.tile([P, BANK], F32, tag="turned", bufs=4)
+            y_bank = psum.tile([P, BANK], F32, tag=("turned", "summed")[m % 2], bufs=4)
             nc.tensor.matmul_mx(
                 y_bank[:],
-                lhsT=w2_w[:, e, 2 * P * m : 2 * P * (m + 1)].bitcast(E2M1),
+                lhsT=w2_w[e][:, 2 * P * m : 2 * P * (m + 1)].bitcast(E2M1),
                 lhsT_scale=w2_s[:, e, P * m : P * (m + 1)],
                 rhs=slot_w[e][:].bitcast(E5M2),
                 rhs_scale=slot_s[e][:],
@@ -131,15 +125,37 @@ def tile_moe_sub_relu2_kernel(
             expert_rows(E - 2, m)
             expert_rows(E - 1, m)
 
+        gate_width = sum(width for g, width in enumerate(GROUPS) if GATE_FIRST[g])
+        held = keep.tile([P, PACK * T + 2 * gate_width], F32, tag="words_then_a", align_bytes=64)
+        a_sb, gate_sb = [], {}
+        used = PACK * T
+        for g, width in enumerate(GROUPS):
+            tokens = slice(starts[g], starts[g] + width)
+            a_g = held[:, PACK * starts[g] : PACK * (starts[g] + width)].rearrange("p (m t) -> p m t", m=PACK)
+            if GATE_FIRST[g]:
+                gate_g = held[:, used : used + 2 * width].rearrange("p (r t) -> p r t", r=2)
+                nc.sync.dma_start(out=gate_g, in_=gate[:, :, tokens].rearrange("r p t -> p r t"))
+                gate_sb[g] = gate_g
+                used = used + 2 * width
+                nc.sync.dma_start(out=a_g, in_=a[:, tokens].rearrange("(p d) t -> p d t", d=PACK))
+            else:
+                nc.sync.dma_start(out=a_g, in_=a[:, tokens].rearrange("(m p) t -> p m t", p=P))
+            a_sb.append(a_g)
+
         da_w = keep.tile([P, T], U32, align_bytes=64)
         da_s = keep.tile([P, T], U8, align_bytes=64)
         slope = {}
+        early_slopes = [g for g in range(len(GROUPS)) if not GATE_FIRST[g]][:NEARLY]
+        early_slope = keep.tile([P, NEARLY, PACK, GROUPS[0]], F32, tag="dy_then_slope", align_bytes=64)
 
         def make_slope(g):
             width = GROUPS[g]
             if GATE_FIRST[g]:
-                slope_g = keep.tile([P, width, PACK], F32, tag=f"slot_s{E - 1}", align_bytes=64)
+                slope_g = ring.tile([P, width, PACK], F32, tag="slot_s", bufs=3, align_bytes=64)
                 nc.scalar.activation(slope_g[:], a_sb[g].rearrange("p d t -> p t d"), RELU, scale=2.0)
+            elif g in early_slopes:
+                slope_g = early_slope[:, early_slopes.index(g)]
+                nc.vector.tensor_scalar(slope_g[:], a_sb[g], 0.0, 2.0, ALU.max, ALU.mult)
             else:
                 slope_g = ring.tile([P, PACK, width], F32, tag="slot_w", bufs=2, align_bytes=64)
                 nc.scalar.activation(slope_g[:], a_sb[g], RELU, scale=2.0)
@@ -147,14 +163,14 @@ def tile_moe_sub_relu2_kernel(
 
         def pick(g, r, m, factor):
             token_list = pos_sb[r][:, starts[g] // LIST_ROWS : (starts[g] + GROUPS[g]) // LIST_ROWS]
-            picked = ring.tile([P, GROUPS[g]], F32, tag=f"picked{r}{m}", bufs=1)
+            picked = ring.tile([P, GROUPS[g]], F32, tag=f"picked{r}{m}", bufs=PICK_BUFS)
             nc.vector.tensor_tensor(picked[:], y[m][:].indirect(token_list), factor, ALU.mult)
             return picked
 
         def transpose_add(target, source, first, last):
             nc.tensor.matmul(target, lhsT=source, rhs=ident[:], is_transpose=True, start=first, stop=last)
 
-        def combine_gate_first(g, da):
+        def combine_gate_first(g):
             width = GROUPS[g]
             turned = [psum.tile([P, BANK], F32, tag="turned", bufs=4, name=f"turned{b}") for b in range(width // P)]
             for m in range(PACK):
@@ -164,12 +180,18 @@ def tile_moe_sub_relu2_kernel(
                         transpose_add(
                             turned[b][:, P * m : P * (m + 1)], picked[r][:, P * b : P * (b + 1)], r == 0, r == 1
                         )
+            sums = []
             for b in range(width // P):
                 dh = ring.tile([P, PACK, P], F32, tag="scaled", bufs=8)
                 nc.scalar.copy(dh[:], turned[b][:].rearrange("p (q d) -> p d q", d=PACK))
-                summed = psum.tile([P, BANK], F32, tag="summed", bufs=2)
+                summed = psum.tile([P, BANK], F32, tag="summed", bufs=4)
                 for d in range(PACK):
                     nc.tensor.transpose(summed[:, P * d : P * (d + 1)], dh[:, d, :], ident[:])
+                sums.append(summed)
+            return sums
+
+        def times_slope(g, sums, da):
+            for b, summed in enumerate(sums):
                 nc.vector.tensor_tensor(
                     da[:, P * b : P * (b + 1), :],
                     summed[:].rearrange("p (d t) -> p t d", d=PACK),
@@ -197,7 +219,7 @@ def tile_moe_sub_relu2_kernel(
                     )
                     scaled[r, b] = scaled_b
             for b in range(width // P):
-                summed = psum.tile([P, BANK], F32, tag="summed", bufs=2)
+                summed = psum.tile([P, BANK], F32, tag="summed", bufs=4)
                 for d in range(PACK):
                     for r in range(2):
                         transpose_add(summed[:, P * d : P * (d + 1)], scaled[r, b][:, d, :], r == 0, r == 1)
@@ -205,9 +227,9 @@ def tile_moe_sub_relu2_kernel(
 
         def project(first, end):
             width = end - first
-            staged = ring.tile([P, K // P, width], F32, tag="staged", bufs=2)
+            staged = ring.tile([P, K // P, width], F32, tag="staged", bufs=4)
             for h in range(K // P):
-                out_bank = psum.tile([P, BANK], F32, tag="out", bufs=2)
+                out_bank = psum.tile([P, BANK], F32, tag="turned", bufs=4)
                 nc.tensor.matmul_mx(
                     out_bank[:],
                     lhsT=w1_w[:, 2 * P * h : 2 * P * (h + 1)].bitcast(E2M1),
@@ -223,24 +245,45 @@ def tile_moe_sub_relu2_kernel(
                     nc.scalar.copy(staged[:, h, :], out_bank[:, BANK - width :])
             nc.sync.dma_start(out=out[:, first:end].rearrange("(h p) t -> p h t", p=P), in_=staged[:])
 
-        stored = 0
+        def quantise(g, da):
+            for first in range(0, GROUPS[g], 2 * P):
+                end = min(first + 2 * P, GROUPS[g])
+                tokens = slice(starts[g] + first, starts[g] + end)
+                nc.vector.quantize_mx(
+                    out=da_w[:, tokens].bitcast(E5M2),
+                    scales=da_s[:, tokens],
+                    in_=da[:, first:end, :].rearrange("p t d -> p (t d)"),
+                )
+
+        def project_behind(g):
+            done = starts[g - LAG + 1] if g >= LAG else 0
+            if done > 0 and done % BANK == 0 and done <= T - BANK:
+                project(done - BANK, done)
+
+        deferred = []
         for g, width in enumerate(GROUPS):
-            start = starts[g]
-            end = start + width
+            end = starts[g] + width
             if g + 1 < len(GROUPS) and not GATE_FIRST[g + 1]:
                 make_slope(g + 1)
-            if GATE_FIRST[g]:
+            if GATE_FIRST[g] or g == 0:
                 make_slope(g)
+            if starts[g] >= T - BANK:
+                deferred.append((g, combine_gate_first(g)))
+                project_behind(g)
+                continue
             da = ring.tile([P, width, PACK], BF16, tag="da", bufs=3, align_bytes=64)
             if GATE_FIRST[g]:
-                combine_gate_first(g, da)
+                times_slope(g, combine_gate_first(g), da)
             else:
                 combine_slope_first(g, da)
-            nc.vector.quantize_mx(
-                out=da_w[:, start:end].bitcast(E5M2),
-                scales=da_s[:, start:end],
-                in_=da[:].rearrange("p t d -> p (t d)"),
-            )
-            if end % BANK == 0 or g == len(GROUPS) - 2:
-                project(stored, end)
-                stored = end
+            quantise(g, da[:])
+            project_behind(g)
+
+        da_last = keep.tile([P, BANK, PACK], BF16, tag=f"y{PACK - 1}", align_bytes=64)
+        for g, sums in deferred:
+            da = da_last[:, starts[g] - (T - BANK) : starts[g] - (T - BANK) + GROUPS[g], :]
+            times_slope(g, sums, da)
+            quantise(g, da)
+            if g == len(GROUPS) - 2:
+                project(T - BANK, starts[g + 1])
+        project(T - GROUPS[-1], T)

@@ -23,11 +23,14 @@ PACK = 4
 BANK = 512
 LIST_ROWS = 16
 BLOCKS = T // P
-GROUPS = (256, 256, 256, 256, 256, 128, 128)
-GATE_FIRST = (False, False, False, True, True, True, True)
+GROUPS = (256, 256, 256, 256, 384, 128)
+KINDS = "ARRRGG"
+GATE_FIRST = tuple(kind != "R" for kind in KINDS)
+F32_MAX = 3.4028234663852886e38
 LAG = 3
+SRELU = False
 EARLY = 2
-NEARLY = 1
+NEARLY = 0
 PICK_BUFS = 2
 RELU = mybir.ActivationFunctionType.Relu
 
@@ -49,18 +52,17 @@ def tile_moe_sub_relu2_kernel(
         offs_sb = keep.tile([P, SLOTS // LIST_ROWS], U16)
         pos_sb = [keep.tile([P, T // LIST_ROWS], U16, name=f"pos{r}") for r in range(2)]
         dy_w = keep.tile([P, T], I32, tag="dy_then_slope", align_bytes=64)
-        dy_s = keep.tile([P, T], U8, align_bytes=64)
+        dy_s = keep.tile([P, T], U8, tag="dy_then_w1", align_bytes=64)
         w2_early = keep.tile([P, EARLY, 2 * H], U8, tag="words_then_a", align_bytes=64)
-        w_s = keep.tile([P, E * H + K], U8, align_bytes=64)
-        w2_s = w_s[:, : E * H].rearrange("p (e i) -> p e i", e=E)
-        w1_s = w_s[:, E * H :]
-        gate_rows = keep.tile([P, P], F32, tag="gate_then_words", align_bytes=64)
+        w2_s = keep.tile([P, E, H], U8, align_bytes=64)
+        gate_rows = [keep.tile([P, P], F32, name=f"gate_rows{r}", tag=f"gate_rows{r}", align_bytes=64) for r in range(2)]
         gate_cols = keep.tile([P, 2 * BLOCKS], F32)
         ident = keep.tile([P, P], F32)
 
         nc.gpsimd.memset(dy_s[:].bitcast(I32), 0)
-        nc.vector.memset(w_s[:].bitcast(I32), 0)
-        nc.gpsimd.memset(gate_rows[:], 0.0)
+        nc.vector.memset(w2_s[:].bitcast(I32), 0)
+        for r in range(2):
+            nc.gpsimd.memset(gate_rows[r][:], 0.0)
 
         nc.sync.dma_start(offs_sb[:], offs)
         nc.sync.dma_start(pos_sb[0][:], pos1)
@@ -69,26 +71,55 @@ def tile_moe_sub_relu2_kernel(
         w2_rows = w2t_words[:, 0].rearrange("e p c -> p e c")
         nc.sync.dma_start(out=w2_early[:].bitcast(I32), in_=w2_rows[:, :EARLY].bitcast(I32))
         load_scale_rows(nc.sync, dy_s[:], dy_scales[0])
-        load_scale_rows(nc.sync, w2_s, w2t_scales[:, 0].rearrange("e b i -> b e i"))
+        load_scale_rows(nc.sync, w2_s[:], w2t_scales[:, 0].rearrange("e b i -> b e i"))
         for r in range(2):
             nc.gpsimd.dma_start(
-                out=gate_rows[r * BLOCKS : (r + 1) * BLOCKS, :], in_=gate[r, 0].rearrange("(b t) -> b t", t=P)
+                out=gate_rows[r][:BLOCKS, :], in_=gate[r, 0].rearrange("(b t) -> b t", t=P)
             )
         make_identity(nc, ident[:])
 
-        gate_bank = psum.tile([P, BANK], F32, tag="turned", bufs=4)
-        nc.tensor.transpose(gate_bank[:, :P], gate_rows[:], ident[:])
-        nc.scalar.activation(gate_cols[:], gate_bank[:, : 2 * BLOCKS], COPY)
-
-        late_words = keep.tile([P, (E - EARLY) * 2 * H + 2 * K], U8, tag="gate_then_words", align_bytes=64)
-        w2_late = late_words[:, : (E - EARLY) * 2 * H].rearrange("p (e c) -> p e c", c=2 * H)
-        w1_w = late_words[:, (E - EARLY) * 2 * H :]
-        nc.sync.dma_start(out=w2_late.bitcast(I32), in_=w2_rows[:, EARLY:].bitcast(I32))
-        load_scale_rows(nc.sync, w1_s, w1t_scales[0])
-        nc.sync.dma_start(out=w1_w.bitcast(I32), in_=w1t_words[0].bitcast(I32))
-        w2_w = [w2_early[:, e, :] if e < EARLY else w2_late[:, e - EARLY, :] for e in range(E)]
+        gate_bank = psum.tile([P, BANK], F32, tag="bank", bufs=8)
+        for r in range(2):
+            nc.tensor.transpose(gate_bank[:, P * r : P * (r + 1)], gate_rows[r][:], ident[:])
+        nc.scalar.activation(
+            gate_cols[:].rearrange("p (r b) -> p r b", r=2),
+            gate_bank[:, : 2 * P].rearrange("p (r b) -> p r b", r=2)[:, :, :BLOCKS],
+            COPY,
+        )
 
         starts = [sum(GROUPS[:g]) for g in range(len(GROUPS))]
+        late_words = keep.tile([P, (E - EARLY) * 2 * H + 2 * K], U8, tag="gate_rows1", align_bytes=64)
+        w2_late = late_words[:, : (E - EARLY) * 2 * H].rearrange("p (e c) -> p e c", c=2 * H)
+        w1_w = late_words[:, (E - EARLY) * 2 * H :]
+        w2_w = [w2_early[:, e, :] if e < EARLY else w2_late[:, e - EARLY, :] for e in range(E)]
+        ahead = [g for g in range(len(GROUPS)) if KINDS[g] == "A"]
+        ahead_in = keep.tile([P, (PACK + 2) * sum(GROUPS[g] for g in ahead)], F32, tag="gate_rows0", align_bytes=64)
+        factor = {}
+        used = 0
+        for g in ahead:
+            width = GROUPS[g]
+            tokens = slice(starts[g], starts[g] + width)
+            a_g = ahead_in[:, used : used + PACK * width].rearrange("p (m t) -> p m t", m=PACK)
+            gate_g = ahead_in[:, used + PACK * width : used + (PACK + 2) * width].rearrange("p (r t) -> p r t", r=2)
+            used = used + (PACK + 2) * width
+            nc.sync.dma_start(out=a_g, in_=a[:, tokens].rearrange("(m p) t -> p m t", p=P))
+            nc.sync.dma_start(out=gate_g, in_=gate[:, :, tokens].rearrange("r p t -> p r t"))
+            if g == ahead[0]:
+                nc.sync.dma_start(out=w2_late.bitcast(I32), in_=w2_rows[:, EARLY:].bitcast(I32))
+            relu_g = ring.tile([P, PACK, width], F32, tag="relu", bufs=2)
+            if g == ahead[0] and SRELU:
+                nc.scalar.activation(relu_g[:], a_g, RELU)
+            else:
+                nc.gpsimd.tensor_scalar(relu_g[:], a_g, F32_MAX, 0.0, ALU.min, ALU.max)
+            for r in range(2):
+                factor_r = keep.tile([P, PACK, width], F32, name=f"factor{g}{r}")
+                nc.gpsimd.tensor_tensor(
+                    factor_r[:], relu_g[:], gate_g[:, r : r + 1, :].to_broadcast([P, PACK, width]), ALU.mult
+                )
+                factor[g, r] = factor_r
+        if not ahead:
+            nc.sync.dma_start(out=w2_late.bitcast(I32), in_=w2_rows[:, EARLY:].bitcast(I32))
+        nc.sync.dma_start(out=w1_w.bitcast(I32), in_=w1t_words[0].bitcast(I32))
 
         y = [keep.tile([P, SLOTS], F32, name=f"y{m}", tag=f"y{m}", align_bytes=64) for m in range(PACK)]
         slot_w, slot_s = [], []
@@ -103,7 +134,7 @@ def tile_moe_sub_relu2_kernel(
             slot_s.append(scales)
 
         def expert_rows(e, m):
-            y_bank = psum.tile([P, BANK], F32, tag=("turned", "summed")[m % 2], bufs=4)
+            y_bank = psum.tile([P, BANK], F32, tag="bank", bufs=8)
             nc.tensor.matmul_mx(
                 y_bank[:],
                 lhsT=w2_w[e][:, 2 * P * m : 2 * P * (m + 1)].bitcast(E2M1),
@@ -125,11 +156,16 @@ def tile_moe_sub_relu2_kernel(
             expert_rows(E - 2, m)
             expert_rows(E - 1, m)
 
+        w1_s = keep.tile([P, K], U8, tag="dy_then_w1", align_bytes=64)
+        nc.gpsimd.memset(w1_s[:].bitcast(I32), 0)
+        load_scale_rows(nc.sync, w1_s[:], w1t_scales[0])
         gate_width = sum(width for g, width in enumerate(GROUPS) if GATE_FIRST[g])
         held = keep.tile([P, PACK * T + 2 * gate_width], F32, tag="words_then_a", align_bytes=64)
-        a_sb, gate_sb = [], {}
+        a_sb, gate_sb = {}, {}
         used = PACK * T
         for g, width in enumerate(GROUPS):
+            if g in ahead:
+                continue
             tokens = slice(starts[g], starts[g] + width)
             a_g = held[:, PACK * starts[g] : PACK * (starts[g] + width)].rearrange("p (m t) -> p m t", m=PACK)
             if GATE_FIRST[g]:
@@ -140,13 +176,13 @@ def tile_moe_sub_relu2_kernel(
                 nc.sync.dma_start(out=a_g, in_=a[:, tokens].rearrange("(p d) t -> p d t", d=PACK))
             else:
                 nc.sync.dma_start(out=a_g, in_=a[:, tokens].rearrange("(m p) t -> p m t", p=P))
-            a_sb.append(a_g)
+            a_sb[g] = a_g
 
         da_w = keep.tile([P, T], U32, align_bytes=64)
         da_s = keep.tile([P, T], U8, align_bytes=64)
         slope = {}
         early_slopes = [g for g in range(len(GROUPS)) if not GATE_FIRST[g]][:NEARLY]
-        early_slope = keep.tile([P, NEARLY, PACK, GROUPS[0]], F32, tag="dy_then_slope", align_bytes=64)
+        early_slope = None
 
         def make_slope(g):
             width = GROUPS[g]
@@ -172,19 +208,22 @@ def tile_moe_sub_relu2_kernel(
 
         def combine_gate_first(g):
             width = GROUPS[g]
-            turned = [psum.tile([P, BANK], F32, tag="turned", bufs=4, name=f"turned{b}") for b in range(width // P)]
+            turned = [psum.tile([P, BANK], F32, tag="bank", bufs=8, name=f"turned{b}") for b in range(width // P)]
             for m in range(PACK):
-                picked = [pick(g, r, m, gate_sb[g][:, r, :]) for r in range(2)]
+                picked = [pick(g, r, m, factor[g, r][:, m, :] if g in ahead else gate_sb[g][:, r, :]) for r in range(2)]
                 for b in range(width // P):
                     for r in range(2):
                         transpose_add(
                             turned[b][:, P * m : P * (m + 1)], picked[r][:, P * b : P * (b + 1)], r == 0, r == 1
                         )
+            return turned
+
+        def turn_sums_back(turned):
             sums = []
-            for b in range(width // P):
+            for b in range(len(turned)):
                 dh = ring.tile([P, PACK, P], F32, tag="scaled", bufs=8)
                 nc.scalar.copy(dh[:], turned[b][:].rearrange("p (q d) -> p d q", d=PACK))
-                summed = psum.tile([P, BANK], F32, tag="summed", bufs=4)
+                summed = psum.tile([P, BANK], F32, tag="bank", bufs=8)
                 for d in range(PACK):
                     nc.tensor.transpose(summed[:, P * d : P * (d + 1)], dh[:, d, :], ident[:])
                 sums.append(summed)
@@ -199,16 +238,48 @@ def tile_moe_sub_relu2_kernel(
                     ALU.mult,
                 )
 
-        def combine_slope_first(g, da):
-            width = GROUPS[g]
-            scaled = {}
+        def round_turned(sums, da):
+            for b, summed in enumerate(sums):
+                da_turned = ring.tile([P, 2, P, 2], BF16, tag="da_turned", bufs=2, align_bytes=64)
+                nc.scalar.activation(
+                    da_turned[:], summed[:].rearrange("p (q u e) -> p u q e", u=2, e=2), COPY, scale=2.0
+                )
+                pairs = da_turned[:].rearrange("p u q e -> p u (q e)").bitcast(F32)
+                back = psum.tile([P, BANK], F32, tag="bank", bufs=8)
+                for u in range(2):
+                    nc.tensor.transpose(back[:, P * u : P * (u + 1)], pairs[:, u, :], ident[:])
+                nc.scalar.copy(
+                    da[:, P * b : P * (b + 1), :].bitcast(F32), back[:, : 2 * P].rearrange("p (u t) -> p t u", u=2)
+                )
+
+        def combine_slope_first(g, da, waiting):
+            blocks = range(GROUPS[g] // P)
+            summed, scaled = {}, {}
+
+            def turn_back(r):
+                for b in blocks:
+                    if r == 0:
+                        summed[b] = psum.tile([P, BANK], F32, tag="bank", bufs=8, name="summed")
+                    for d in range(PACK):
+                        transpose_add(
+                            summed[b][:, P * d : P * (d + 1)],
+                            scaled[r, b][:, d, :],
+                            r == 0 and d == 0,
+                            r == 1 and d == PACK - 1,
+                        )
+
             for r in range(2):
-                turned = [psum.tile([P, BANK], F32, tag="turned", bufs=4, name=f"turned{b}") for b in range(width // P)]
+                turned = [psum.tile([P, BANK], F32, tag="bank", bufs=8, name=f"turned{b}") for b in blocks]
                 for m in range(PACK):
                     picked = pick(g, r, m, slope[g][:, m, :])
-                    for b in range(width // P):
+                    for b in blocks:
                         nc.tensor.transpose(turned[b][:, P * m : P * (m + 1)], picked[:, P * b : P * (b + 1)], ident[:])
-                for b in range(width // P):
+                if r == 0:
+                    for before, turned_before in waiting:
+                        finish(before, turned_before)
+                if r == 1:
+                    turn_back(0)
+                for b in blocks:
                     scaled_b = ring.tile([P, PACK, P], F32, tag="scaled", bufs=8)
                     column = r * BLOCKS + starts[g] // P + b
                     nc.scalar.activation(
@@ -218,18 +289,16 @@ def tile_moe_sub_relu2_kernel(
                         scale=gate_cols[:, column : column + 1],
                     )
                     scaled[r, b] = scaled_b
-            for b in range(width // P):
-                summed = psum.tile([P, BANK], F32, tag="summed", bufs=4)
-                for d in range(PACK):
-                    for r in range(2):
-                        transpose_add(summed[:, P * d : P * (d + 1)], scaled[r, b][:, d, :], r == 0, r == 1)
-                nc.scalar.copy(da[:, P * b : P * (b + 1), :], summed[:].rearrange("p (d t) -> p t d", d=PACK))
+                if r == 1:
+                    turn_back(r)
+            for b in blocks:
+                nc.scalar.copy(da[:, P * b : P * (b + 1), :], summed[b][:].rearrange("p (d t) -> p t d", d=PACK))
 
         def project(first, end):
             width = end - first
             staged = ring.tile([P, K // P, width], F32, tag="staged", bufs=4)
             for h in range(K // P):
-                out_bank = psum.tile([P, BANK], F32, tag="turned", bufs=4)
+                out_bank = psum.tile([P, BANK], F32, tag="bank", bufs=8)
                 nc.tensor.matmul_mx(
                     out_bank[:],
                     lhsT=w1_w[:, 2 * P * h : 2 * P * (h + 1)].bitcast(E2M1),
@@ -257,28 +326,41 @@ def tile_moe_sub_relu2_kernel(
 
         def project_behind(g):
             done = starts[g - LAG + 1] if g >= LAG else 0
-            if done > 0 and done % BANK == 0 and done <= T - BANK:
+            if done > 0 and done % BANK == 0 and done < T - BANK:
                 project(done - BANK, done)
 
-        deferred = []
-        for g, width in enumerate(GROUPS):
-            end = starts[g] + width
-            if g + 1 < len(GROUPS) and not GATE_FIRST[g + 1]:
-                make_slope(g + 1)
-            if GATE_FIRST[g] or g == 0:
-                make_slope(g)
-            if starts[g] >= T - BANK:
-                deferred.append((g, combine_gate_first(g)))
-                project_behind(g)
-                continue
-            da = ring.tile([P, width, PACK], BF16, tag="da", bufs=3, align_bytes=64)
-            if GATE_FIRST[g]:
-                times_slope(g, combine_gate_first(g), da)
-            else:
-                combine_slope_first(g, da)
-            quantise(g, da[:])
-            project_behind(g)
+        deferred, waiting = [], []
 
+        def finish(g, turned):
+            if KINDS[g] == "G" and starts[g] >= T - BANK:
+                deferred.append((g, turn_sums_back(turned)))
+                return
+            da = ring.tile([P, GROUPS[g], PACK], BF16, tag="da", bufs=3, align_bytes=64)
+            if KINDS[g] == "A":
+                round_turned(turned, da)
+            else:
+                times_slope(g, turn_sums_back(turned), da)
+            quantise(g, da[:])
+
+        for g, width in enumerate(GROUPS):
+            if g + 1 < len(GROUPS) and KINDS[g + 1] == "R":
+                make_slope(g + 1)
+            if KINDS[g] == "G" or (g == 0 and KINDS[g] == "R"):
+                make_slope(g)
+            if KINDS[g] == "R":
+                da = ring.tile([P, width, PACK], BF16, tag="da", bufs=3, align_bytes=64)
+                combine_slope_first(g, da, waiting)
+                waiting = []
+                quantise(g, da[:])
+            else:
+                turned = combine_gate_first(g)
+                for before, turned_before in waiting:
+                    finish(before, turned_before)
+                waiting = [(g, turned)]
+            project_behind(g)
+        for before, turned_before in waiting:
+            finish(before, turned_before)
+        project(T - 2 * BANK, T - BANK)
         da_last = keep.tile([P, BANK, PACK], BF16, tag=f"y{PACK - 1}", align_bytes=64)
         for g, sums in deferred:
             da = da_last[:, starts[g] - (T - BANK) : starts[g] - (T - BANK) + GROUPS[g], :]

from contextlib import ExitStack

import concourse.mybir as mybir
from concourse.masks import make_identity

K, T, E, C, H, N = 256, 1536, 6, 512, 512, 512
SLOTS = E * C
FLOPS = 2 * N * H * SLOTS + 2 * H * K * T

F32 = mybir.dt.float32
BF16 = mybir.dt.bfloat16
I32 = mybir.dt.int32
U32 = mybir.dt.uint32
U16 = mybir.dt.uint16
U8 = mybir.dt.uint8
E5M2 = mybir.dt.float8_e5m2_x4
E2M1 = mybir.dt.float4_e2m1fn_x4
ALU = mybir.AluOpType
COPY = mybir.ActivationFunctionType.Copy

P = 128
PACK = 4
BANK = 512
LIST_ROWS = 16
BLOCKS = T // P
GROUPS = (256, 256, 256, 256, 384, 128)
KINDS = "ARRRGG"
GATE_FIRST = tuple(kind != "R" for kind in KINDS)
F32_MAX = 3.4028234663852886e38
LAG = 3
SRELU = False
EARLY = 2
NEARLY = 0
PICK_BUFS = 2
RELU = mybir.ActivationFunctionType.Relu


def load_scale_rows(queue, plane, rows):
    for r in range(4):
        queue.dma_start(out=plane[r:P:32].bitcast(I32), in_=rows[r:16:4].bitcast(I32))


def tile_moe_sub_relu2_kernel(
    tc, dy_words, dy_scales, w2t_words, w2t_scales, w1t_words, w1t_scales, a, gate, offs, pos1, pos2, out
):
    nc = tc.nc
    with ExitStack() as ctx:
        keep = ctx.enter_context(tc.tile_pool(name="keep", bufs=1))
        ring = ctx.enter_context(tc.tile_pool(name="ring", bufs=1))
        psum = ctx.enter_context(tc.psum_pool(name="psum", bufs=1))

        offs_sb = keep.tile([P, SLOTS // LIST_ROWS], U16)
        pos_sb = [keep.tile([P, T // LIST_ROWS], U16, name=f"pos{r}") for r in range(2)]
        dy_w = keep.tile([P, T], I32, tag="dy_then_slope", align_bytes=64)
        dy_s = keep.tile([P, T], U8, tag="dy_then_w1", align_bytes=64)
        w2_early = keep.tile([P, EARLY, 2 * H], U8, tag="words_then_a", align_bytes=64)
        w2_s = keep.tile([P, E, H], U8, align_bytes=64)
        gate_rows = [keep.tile([P, P], F32, name=f"gate_rows{r}", tag=f"gate_rows{r}", align_bytes=64) for r in range(2)]
        gate_cols = keep.tile([P, 2 * BLOCKS], F32)
        ident = keep.tile([P, P], F32)

        nc.gpsimd.memset(dy_s[:].bitcast(I32), 0)
        nc.vector.memset(w2_s[:].bitcast(I32), 0)
        for r in range(2):
            nc.gpsimd.memset(gate_rows[r][:], 0.0)

        nc.sync.dma_start(offs_sb[:], offs)
        nc.sync.dma_start(pos_sb[0][:], pos1)
        nc.sync.dma_start(pos_sb[1][:], pos2)
        nc.sync.dma_start(out=dy_w[:], in_=dy_words[0].rearrange("p t d -> p (t d)").bitcast(I32))
        w2_rows = w2t_words[:, 0].rearrange("e p c -> p e c")
        nc.sync.dma_start(out=w2_early[:].bitcast(I32), in_=w2_rows[:, :EARLY].bitcast(I32))
        load_scale_rows(nc.sync, dy_s[:], dy_scales[0])
        load_scale_rows(nc.sync, w2_s[:], w2t_scales[:, 0].rearrange("e b i -> b e i"))
        for r in range(2):
            nc.gpsimd.dma_start(
                out=gate_rows[r][:BLOCKS, :], in_=gate[r, 0].rearrange("(b t) -> b t", t=P)
            )
        make_identity(nc, ident[:])

        gate_bank = psum.tile([P, BANK], F32, tag="bank", bufs=8)
        for r in range(2):
            nc.tensor.transpose(gate_bank[:, P * r : P * (r + 1)], gate_rows[r][:], ident[:])
        nc.scalar.activation(
            gate_cols[:].rearrange("p (r b) -> p r b", r=2),
            gate_bank[:, : 2 * P].rearrange("p (r b) -> p r b", r=2)[:, :, :BLOCKS],
            COPY,
        )

        starts = [sum(GROUPS[:g]) for g in range(len(GROUPS))]
        late_words = keep.tile([P, (E - EARLY) * 2 * H + 2 * K], U8, tag="gate_rows1", align_bytes=64)
        w2_late = late_words[:, : (E - EARLY) * 2 * H].rearrange("p (e c) -> p e c", c=2 * H)
        w1_w = late_words[:, (E - EARLY) * 2 * H :]
        w2_w = [w2_early[:, e, :] if e < EARLY else w2_late[:, e - EARLY, :] for e in range(E)]
        ahead = [g for g in range(len(GROUPS)) if KINDS[g] == "A"]
        ahead_in = keep.tile([P, (PACK + 2) * sum(GROUPS[g] for g in ahead)], F32, tag="gate_rows0", align_bytes=64)
        factor = {}
        used = 0
        for g in ahead:
            width = GROUPS[g]
            tokens = slice(starts[g], starts[g] + width)
            a_g = ahead_in[:, used : used + PACK * width].rearrange("p (m t) -> p m t", m=PACK)
            gate_g = ahead_in[:, used + PACK * width : used + (PACK + 2) * width].rearrange("p (r t) -> p r t", r=2)
            used = used + (PACK + 2) * width
            nc.sync.dma_start(out=a_g, in_=a[:, tokens].rearrange("(m p) t -> p m t", p=P))
            nc.sync.dma_start(out=gate_g, in_=gate[:, :, tokens].rearrange("r p t -> p r t"))
            if g == ahead[0]:
                nc.sync.dma_start(out=w2_late.bitcast(I32), in_=w2_rows[:, EARLY:].bitcast(I32))
            relu_g = ring.tile([P, PACK, width], F32, tag="relu", bufs=2)
            if g == ahead[0] and SRELU:
                nc.scalar.activation(relu_g[:], a_g, RELU)
            else:
                nc.gpsimd.tensor_scalar(relu_g[:], a_g, F32_MAX, 0.0, ALU.min, ALU.max)
            for r in range(2):
                factor_r = keep.tile([P, PACK, width], F32, name=f"factor{g}{r}")
                nc.gpsimd.tensor_tensor(
                    factor_r[:], relu_g[:], gate_g[:, r : r + 1, :].to_broadcast([P, PACK, width]), ALU.mult
                )
                factor[g, r] = factor_r
        if not ahead:
            nc.sync.dma_start(out=w2_late.bitcast(I32), in_=w2_rows[:, EARLY:].bitcast(I32))
        nc.sync.dma_start(out=w1_w.bitcast(I32), in_=w1t_words[0].bitcast(I32))

        y = [keep.tile([P, SLOTS], F32, name=f"y{m}", tag=f"y{m}", align_bytes=64) for m in range(PACK)]
        slot_w, slot_s = [], []

        def gather_expert(e):
            slot_list = offs_sb[:, e * C // LIST_ROWS : (e + 1) * C // LIST_ROWS]
            words = ring.tile([P, C], U32, tag="slot_w", bufs=2, align_bytes=64)
            scales = ring.tile([P, C], U8, tag="slot_s", bufs=3, align_bytes=64)
            nc.vector.tensor_copy(words[:], dy_w[:].bitcast(U32).indirect(slot_list))
            nc.vector.tensor_copy(scales[:], dy_s[:].indirect(slot_list))
            slot_w.append(words)
            slot_s.append(scales)

        def expert_rows(e, m):
            y_bank = psum.tile([P, BANK], F32, tag="bank", bufs=8)
            nc.tensor.matmul_mx(
                y_bank[:],
                lhsT=w2_w[e][:, 2 * P * m : 2 * P * (m + 1)].bitcast(E2M1),
                lhsT_scale=w2_s[:, e, P * m : P * (m + 1)],
                rhs=slot_w[e][:].bitcast(E5M2),
                rhs_scale=slot_s[e][:],
                start=True,
                stop=True,
            )
            nc.scalar.copy(y[m][:, e * C : (e + 1) * C], y_bank[:])

        for e in range(E - 2):
            gather_expert(e)
            for m in range(PACK):
                expert_rows(e, m)
        gather_expert(E - 2)
        gather_expert(E - 1)
        for m in range(PACK):
            expert_rows(E - 2, m)
            expert_rows(E - 1, m)

        w1_s = keep.tile([P, K], U8, tag="dy_then_w1", align_bytes=64)
        nc.gpsimd.memset(w1_s[:].bitcast(I32), 0)
        load_scale_rows(nc.sync, w1_s[:], w1t_scales[0])
        gate_width = sum(width for g, width in enumerate(GROUPS) if GATE_FIRST[g])
        held = keep.tile([P, PACK * T + 2 * gate_width], F32, tag="words_then_a", align_bytes=64)
        a_sb, gate_sb = {}, {}
        used = PACK * T
        for g, width in enumerate(GROUPS):
            if g in ahead:
                continue
            tokens = slice(starts[g], starts[g] + width)
            a_g = held[:, PACK * starts[g] : PACK * (starts[g] + width)].rearrange("p (m t) -> p m t", m=PACK)
            if GATE_FIRST[g]:
                gate_g = held[:, used : used + 2 * width].rearrange("p (r t) -> p r t", r=2)
                nc.sync.dma_start(out=gate_g, in_=gate[:, :, tokens].rearrange("r p t -> p r t"))
                gate_sb[g] = gate_g
                used = used + 2 * width
                nc.sync.dma_start(out=a_g, in_=a[:, tokens].rearrange("(p d) t -> p d t", d=PACK))
            else:
                nc.sync.dma_start(out=a_g, in_=a[:, tokens].rearrange("(m p) t -> p m t", p=P))
            a_sb[g] = a_g

        da_w = keep.tile([P, T], U32, align_bytes=64)
        da_s = keep.tile([P, T], U8, align_bytes=64)
        slope = {}
        early_slopes = [g for g in range(len(GROUPS)) if not GATE_FIRST[g]][:NEARLY]
        early_slope = None

        def make_slope(g):
            width = GROUPS[g]
            if GATE_FIRST[g]:
                slope_g = ring.tile([P, width, PACK], F32, tag="slot_s", bufs=3, align_bytes=64)
                nc.scalar.activation(slope_g[:], a_sb[g].rearrange("p d t -> p t d"), RELU, scale=2.0)
            elif g in early_slopes:
                slope_g = early_slope[:, early_slopes.index(g)]
                nc.vector.tensor_scalar(slope_g[:], a_sb[g], 0.0, 2.0, ALU.max, ALU.mult)
            else:
                slope_g = ring.tile([P, PACK, width], F32, tag="slot_w", bufs=2, align_bytes=64)
                nc.scalar.activation(slope_g[:], a_sb[g], RELU, scale=2.0)
            slope[g] = slope_g

        def pick(g, r, m, factor):
            token_list = pos_sb[r][:, starts[g] // LIST_ROWS : (starts[g] + GROUPS[g]) // LIST_ROWS]
            picked = ring.tile([P, GROUPS[g]], F32, tag=f"picked{r}{m}", bufs=PICK_BUFS)
            nc.vector.tensor_tensor(picked[:], y[m][:].indirect(token_list), factor, ALU.mult)
            return picked

        def transpose_add(target, source, first, last):
            nc.tensor.matmul(target, lhsT=source, rhs=ident[:], is_transpose=True, start=first, stop=last)

        def combine_gate_first(g):
            width = GROUPS[g]
            turned = [psum.tile([P, BANK], F32, tag="bank", bufs=8, name=f"turned{b}") for b in range(width // P)]
            for m in range(PACK):
                picked = [pick(g, r, m, factor[g, r][:, m, :] if g in ahead else gate_sb[g][:, r, :]) for r in range(2)]
                for b in range(width // P):
                    for r in range(2):
                        transpose_add(
                            turned[b][:, P * m : P * (m + 1)], picked[r][:, P * b : P * (b + 1)], r == 0, r == 1
                        )
            return turned

        def turn_sums_back(turned):
            sums = []
            for b in range(len(turned)):
                dh = ring.tile([P, PACK, P], F32, tag="scaled", bufs=8)
                nc.scalar.copy(dh[:], turned[b][:].rearrange("p (q d) -> p d q", d=PACK))
                summed = psum.tile([P, BANK], F32, tag="bank", bufs=8)
                for d in range(PACK):
                    nc.tensor.transpose(summed[:, P * d : P * (d + 1)], dh[:, d, :], ident[:])
                sums.append(summed)
            return sums

        def times_slope(g, sums, da):
            for b, summed in enumerate(sums):
                nc.vector.tensor_tensor(
                    da[:, P * b : P * (b + 1), :],
                    summed[:].rearrange("p (d t) -> p t d", d=PACK),
                    slope[g][:, P * b : P * (b + 1), :],
                    ALU.mult,
                )

        def round_turned(sums, da):
            for b, summed in enumerate(sums):
                da_turned = ring.tile([P, 2, P, 2], BF16, tag="da_turned", bufs=2, align_bytes=64)
                nc.scalar.activation(
                    da_turned[:], summed[:].rearrange("p (q u e) -> p u q e", u=2, e=2), COPY, scale=2.0
                )
                pairs = da_turned[:].rearrange("p u q e -> p u (q e)").bitcast(F32)
                back = psum.tile([P, BANK], F32, tag="bank", bufs=8)
                for u in range(2):
                    nc.tensor.transpose(back[:, P * u : P * (u + 1)], pairs[:, u, :], ident[:])
                nc.scalar.copy(
                    da[:, P * b : P * (b + 1), :].bitcast(F32), back[:, : 2 * P].rearrange("p (u t) -> p t u", u=2)
                )

        def combine_slope_first(g, da, waiting):
            blocks = range(GROUPS[g] // P)
            summed, scaled = {}, {}

            def turn_back(r):
                for b in blocks:
                    if r == 0:
                        summed[b] = psum.tile([P, BANK], F32, tag="bank", bufs=8, name="summed")
                    for d in range(PACK):
                        transpose_add(
                            summed[b][:, P * d : P * (d + 1)],
                            scaled[r, b][:, d, :],
                            r == 0 and d == 0,
                            r == 1 and d == PACK - 1,
                        )

            for r in range(2):
                turned = [psum.tile([P, BANK], F32, tag="bank", bufs=8, name=f"turned{b}") for b in blocks]
                for m in range(PACK):
                    picked = pick(g, r, m, slope[g][:, m, :])
                    for b in blocks:
                        nc.tensor.transpose(turned[b][:, P * m : P * (m + 1)], picked[:, P * b : P * (b + 1)], ident[:])
                if r == 0:
                    for before, turned_before in waiting:
                        finish(before, turned_before)
                if r == 1:
                    turn_back(0)
                for b in blocks:
                    scaled_b = ring.tile([P, PACK, P], F32, tag="scaled", bufs=8)
                    column = r * BLOCKS + starts[g] // P + b
                    nc.scalar.activation(
                        scaled_b[:],
                        turned[b][:].rearrange("p (q d) -> p d q", d=PACK),
                        COPY,
                        scale=gate_cols[:, column : column + 1],
                    )
                    scaled[r, b] = scaled_b
                if r == 1:
                    turn_back(r)
            for b in blocks:
                nc.scalar.copy(da[:, P * b : P * (b + 1), :], summed[b][:].rearrange("p (d t) -> p t d", d=PACK))

        def project(first, end):
            width = end - first
            staged = ring.tile([P, K // P, width], F32, tag="staged", bufs=4)
            for h in range(K // P):
                out_bank = psum.tile([P, BANK], F32, tag="bank", bufs=8)
                nc.tensor.matmul_mx(
                    out_bank[:],
                    lhsT=w1_w[:, 2 * P * h : 2 * P * (h + 1)].bitcast(E2M1),
                    lhsT_scale=w1_s[:, P * h : P * (h + 1)],
                    rhs=da_w[:, end - BANK : end].bitcast(E5M2),
                    rhs_scale=da_s[:, end - BANK : end],
                    start=True,
                    stop=True,
                )
                if end == T and h == 1:
                    nc.vector.tensor_copy(staged[:, h, :], out_bank[:, BANK - width :])
                else:
                    nc.scalar.copy(staged[:, h, :], out_bank[:, BANK - width :])
            nc.sync.dma_start(out=out[:, first:end].rearrange("(h p) t -> p h t", p=P), in_=staged[:])

        def quantise(g, da):
            for first in range(0, GROUPS[g], 2 * P):
                end = min(first + 2 * P, GROUPS[g])
                tokens = slice(starts[g] + first, starts[g] + end)
                nc.vector.quantize_mx(
                    out=da_w[:, tokens].bitcast(E5M2),
                    scales=da_s[:, tokens],
                    in_=da[:, first:end, :].rearrange("p t d -> p (t d)"),
                )

        def project_behind(g):
            done = starts[g - LAG + 1] if g >= LAG else 0
            if done > 0 and done % BANK == 0 and done < T - BANK:
                project(done - BANK, done)

        deferred, waiting = [], []

        def finish(g, turned):
            if KINDS[g] == "G" and starts[g] >= T - BANK:
                deferred.append((g, turn_sums_back(turned)))
                return
            da = ring.tile([P, GROUPS[g], PACK], BF16, tag="da", bufs=3, align_bytes=64)
            if KINDS[g] == "A":
                round_turned(turned, da)
            else:
                times_slope(g, turn_sums_back(turned), da)
            quantise(g, da[:])

        for g, width in enumerate(GROUPS):
            if g + 1 < len(GROUPS) and KINDS[g + 1] == "R":
                make_slope(g + 1)
            if KINDS[g] == "G" or (g == 0 and KINDS[g] == "R"):
                make_slope(g)
            if KINDS[g] == "R":
                da = ring.tile([P, width, PACK], BF16, tag="da", bufs=3, align_bytes=64)
                combine_slope_first(g, da, waiting)
                waiting = []
                quantise(g, da[:])
            else:
                turned = combine_gate_first(g)
                for before, turned_before in waiting:
                    finish(before, turned_before)
                waiting = [(g, turned)]
            project_behind(g)
        for before, turned_before in waiting:
            finish(before, turned_before)
        project(T - 2 * BANK, T - BANK)
        da_last = keep.tile([P, BANK, PACK], BF16, tag=f"y{PACK - 1}", align_bytes=64)
        for g, sums in deferred:
            da = da_last[:, starts[g] - (T - BANK) : starts[g] - (T - BANK) + GROUPS[g], :]
            times_slope(g, sums, da)
            quantise(g, da)
            if g == len(GROUPS) - 2:
                project(T - BANK, starts[g + 1])
        project(T - GROUPS[-1], T)
